import numpy as np
import ml_dtypes


def mxq(x, axis, fmt="e4m3"):
    dtype, down = {"e4m3": (ml_dtypes.float8_e4m3fn, 7), "e5m2": (ml_dtypes.float8_e5m2, 14)}[fmt]
    v = np.moveaxis(np.asarray(x, np.float32).astype(ml_dtypes.bfloat16).astype(np.float64), axis, -1)
    blocks = v.reshape(v.shape[:-1] + (-1, 32))
    amax = np.abs(blocks).max(-1, keepdims=True)
    byte = np.maximum(np.where(amax > 0, np.frexp(amax)[1] - 1 + 127, 0) - down, 1)
    scale = np.exp2(byte - 127.0)
    codes = (blocks / scale).astype(np.float32).astype(dtype).astype(np.float64)
    return np.moveaxis((codes * scale).reshape(v.shape), -1, axis)


WIDE = False


def mx_kscale(k):
    if not WIDE:
        return np.ones(k)
    levels = np.array([10, -10, 5, -5, 0])
    if k % 512:
        return np.exp2(np.random.permutation(np.resize(levels, k // 32))).repeat(32)
    a = np.empty((k // 512, 16))
    for p in range(k // 512):
        a[p, :8] = np.random.permutation(np.resize(levels, 8))
        for g in range(8):
            far = levels[np.abs(levels - a[p, g]) >= 10]
            a[p, g + 8] = far[np.random.randint(len(far))]
    return np.exp2(a.ravel()).repeat(32)


BF16 = ml_dtypes.bfloat16


def bf(x):
    return np.asarray(x, np.float32).astype(BF16)


def f64(x):
    return np.asarray(x).astype(np.float64)


T, D, C, L, V, J = 1024, 1024, 128, 16, 2048, 512


def setup_inputs():
    s, u = mx_kscale(D), mx_kscale(T)
    return {"x": bf(np.random.standard_normal((T, D)) * s),
            "w_word": bf(0.7 * np.random.standard_normal((D, V)) / np.sqrt(D) / s[:, None]),
            "b_word": bf(0.5 * np.random.standard_normal(V)),
            "w_cluster": bf(0.7 * np.random.standard_normal((D, C)) / np.sqrt(D) / s[:, None]),
            "b_cluster": bf(0.5 * np.random.standard_normal(C)),
            "importance": bf((1 + 0.2 * np.random.standard_normal(T)) * u),
            "pool": bf(np.random.standard_normal((J, T)) / np.sqrt(T) / u),
            "idf": bf(1 + 0.1 * np.random.standard_normal(V))}


def softmax_last(z):
    e = np.exp(z - z.max(axis=-1, keepdims=True))
    return e / e.sum(axis=-1, keepdims=True)


def reference(x, w_word, b_word, w_cluster, b_cluster, importance, pool, idf):
    xq = mxq(f64(x), 1, "e4m3")
    zw = (xq @ mxq(f64(w_word), 0, "e4m3")) + f64(b_word)
    zc = (xq @ mxq(f64(w_cluster), 0, "e4m3")) + f64(b_cluster)
    inside = softmax_last(zw.reshape(T, C, L)) * L
    gate = softmax_last(zc) * C
    lift = (gate[:, :, None] * inside).reshape(T, V)
    h = lift * f64(importance)[:, None]
    pooled = mxq(f64(pool), 1, "e4m3") @ mxq(h, 0, "e4m3")
    return pooled * f64(idf)

@@ -1,0 +1,450 @@
+from contextlib import ExitStack
+
+import concourse.mybir as mybir
+from concourse.masks import make_identity
+
+T, D, C, L, V, J = 1024, 1024, 128, 16, 2048, 512
+FLOPS = 2 * T * D * (V + C) + 2 * J * T * V
+
+F32 = mybir.dt.float32
+BF16 = mybir.dt.bfloat16
+U32 = mybir.dt.uint32
+U8 = mybir.dt.uint8
+FP8X4 = mybir.dt.float8_e4m3fn_x4
+ALU = mybir.AluOpType
+ACT = mybir.ActivationFunctionType
+AXIS = mybir.AxisListType
+
+P = 128
+PACK = 4
+PASS = P * PACK
+CHUNK = 512
+N_CHUNKS = V // CHUNK
+N_GROUPS = T // PASS
+N_PASSES = D // PASS
+BLOCKS = CHUNK // P
+N_UNITS = N_CHUNKS * N_GROUPS
+N_TILES = N_UNITS * BLOCKS
+CHUNK_CLUSTERS = CHUNK // L
+BLOCK_CLUSTERS = P // L
+PIECE = CHUNK // 2
+J_TILES = J // P
+
+
+def tile_hierarchical_softmax_pooling_f4_kernel(
+    tc, x, w_word, b_word, w_cluster, b_cluster, importance, pool, idf, out
+):
+    nc = tc.nc
+    with ExitStack() as ctx:
+        keep = ctx.enter_context(tc.tile_pool(name="keep", bufs=1))
+        work = ctx.enter_context(tc.tile_pool(name="work", bufs=2))
+        psum = ctx.enter_context(tc.psum_pool(name="psum", bufs=1))
+        ctx.enter_context(tc.manual_schedule())
+
+        def bank(tag, shape, dtype=F32):
+            depth = {"mx": 2, "z": 3, "sum": 1, "out": 2}[tag]
+            return psum.tile(shape, dtype, name="bank_" + tag, tag=tag, bufs=depth)
+
+        def mx_operand(name, columns):
+            codes = keep.tile([P, columns], U32, name=name + "_codes", align_bytes=64)
+            scales = keep.tile([P, columns], U8, name=name + "_scales", align_bytes=64)
+            return codes, scales
+
+        def quantize(operand, grouped):
+            codes, scales = operand
+            nc.vector.quantize_mx(out=codes[:].bitcast(FP8X4), scales=scales[:], in_=grouped)
+
+        def mx_pass(acc, stationary, m0, moving, n0, width, first, last):
+            nc.tensor.matmul_mx(
+                out=acc,
+                lhsT=stationary[0][:, m0 : m0 + P].bitcast(FP8X4),
+                lhsT_scale=stationary[1][:, m0 : m0 + P],
+                rhs=moving[0][:, n0 : n0 + width].bitcast(FP8X4),
+                rhs_scale=moving[1][:, n0 : n0 + width],
+                start=first,
+                stop=last,
+            )
+
+        bias_rows = keep.tile([P, P], BF16, name="bias_rows")
+        nc.gpsimd.memset(bias_rows[:], 0.0)
+        ident = keep.tile([P, P], F32, name="ident")
+        make_identity(nc, ident[:])
+        ident_bf = keep.tile([P, P], BF16, name="ident_bf")
+        make_identity(nc, ident_bf[:])
+
+        x_raw = {}
+        w_raw = {}
+
+        def load_x(g, k):
+            x_raw[g, k] = keep.tile([P, PACK, PASS], BF16, name="x_raw_%d_%d" % (g, k))
+            rows = x[g * PASS : (g + 1) * PASS, k * PASS : (k + 1) * PASS]
+            nc.sync.dma_start(out=x_raw[g, k][:], in_=rows.rearrange("(p t) d -> p t d", t=PACK))
+
+        def load_w(k, v0, width):
+            raw = keep.tile([P, PACK, width], BF16, name="w_raw_%d_%d" % (k, v0))
+            rows = w_word[k * PASS : (k + 1) * PASS, v0 : v0 + width]
+            nc.sync.dma_start(out=raw[:], in_=rows.rearrange("(p j) v -> p j v", j=PACK))
+            for c0 in range(0, width, PIECE):
+                w_raw[k, (v0 + c0) // PIECE] = raw[:, :, c0 : c0 + PIECE]
+
+        for k in range(N_PASSES):
+            load_x(0, k)
+            load_w(k, 0, PIECE)
+        nc.scalar.dma_start(out=bias_rows[0 : V // P, :], in_=b_word.rearrange("(q p) -> q p", p=P))
+        nc.scalar.dma_start(out=bias_rows[V // P : V // P + 1, :], in_=b_cluster.rearrange("(q p) -> q p", p=P))
+        for k in range(N_PASSES):
+            load_w(k, PIECE, PIECE)
+        for k in range(N_PASSES):
+            load_x(1, k)
+        wc_raw = keep.tile([P, N_PASSES, PACK, C], BF16, name="wc_raw")
+        nc.sync.dma_start(
+            out=wc_raw[:].rearrange("p k j c -> p k (j c)"),
+            in_=w_cluster.rearrange("(k p j) c -> p k (j c)", p=P, j=PACK),
+        )
+        for k in range(N_PASSES):
+            load_w(k, CHUNK, CHUNK)
+        imp = keep.tile([P, N_GROUPS, PACK], BF16, name="imp")
+        nc.sync.dma_start(out=imp[:], in_=importance.rearrange("(g p t) -> p g t", p=P, t=PACK))
+        pool_raw = keep.tile([P, J_TILES, T], BF16, name="pool_raw")
+        nc.sync.dma_start(out=pool_raw[:], in_=pool.rearrange("(jt j) t -> j jt t", j=P))
+        for k in range(N_PASSES):
+            load_w(k, 2 * CHUNK, CHUNK)
+        idf_rows = keep.tile([P, V], BF16, name="idf_rows")
+        nc.sync.dma_start(out=idf_rows[:], in_=idf.partition_broadcast(P))
+        for k in range(N_PASSES):
+            load_w(k, 3 * CHUNK, CHUNK)
+
+        x_mx = {}
+        x_grouped = {}
+
+        def copy_on(engine, dst, src):
+            if engine == "vector":
+                nc.vector.tensor_copy(out=dst, in_=src)
+            else:
+                nc.scalar.copy(out=dst, in_=src)
+
+        def turn_x(g, k, tags, engines):
+            grouped = work.tile([P, PACK, P, 2], F32, name="x_grouped", align_bytes=64)
+            x_grouped[g, k] = grouped
+            words = x_raw[g, k][:].bitcast(F32)
+            for half in range(2):
+                turned = bank(tags[half], [P, 2, 2, P])
+                for t in range(2):
+                    for u in range(2):
+                        nc.tensor.transpose(turned[:, t, u, :], words[:, 2 * half + t, u::2], ident[:])
+                copy_on(engines[half], grouped[:, 2 * half : 2 * half + 2, :, :], turned[:].rearrange("p t u r -> p t r u"))
+
+        def quantize_x(g, k):
+            x_mx[g, k] = mx_operand("x_%d_%d" % (g, k), PASS)
+            quantize(x_mx[g, k], x_grouped[g, k][:].rearrange("p t r u -> p (t r u)").bitcast(BF16))
+
+        w_grouped = {}
+        w_mx = {}
+
+        def interleave(engine, dst, src):
+            copy_on(engine, dst.rearrange("p (c i) j -> p c j i", i=4), src.rearrange("p j (c i) -> p c j i", i=4))
+
+        def interleave_w(piece, k, c0, width, engine):
+            if piece not in w_grouped:
+                w_grouped[piece] = work.tile([P, N_PASSES, PIECE, PACK], BF16, name="w_grouped", align_bytes=64)
+            interleave(engine, w_grouped[piece][:, k, c0 : c0 + width, :], w_raw[k, piece][:, :, c0 : c0 + width])
+
+        def quantize_w(piece):
+            w_mx[piece] = mx_operand("w_%d" % piece, N_PASSES * PIECE)
+            quantize(w_mx[piece], w_grouped[piece][:].rearrange("p k v j -> p (k v j)"))
+
+        bias = keep.tile([P, 32], F32, name="bias")
+        logits = {}
+        biased = {}
+        turned_z = {}
+        top = {}
+        shifted = {}
+        expd = {}
+
+        def logits_mx(key, stationary, m0, m_step, g):
+            logits[key] = bank("mx", [P, PASS])
+            for k in range(N_PASSES):
+                mx_pass(logits[key][:], stationary, m0 + k * m_step, x_mx[g, k], 0, PASS, k == 0, k == N_PASSES - 1)
+
+        def word_mx(i):
+            u, q = divmod(i, BLOCKS)
+            n, g = divmod(u, N_GROUPS)
+            logits_mx(i, w_mx[2 * n + q // 2], (q % 2) * P, PIECE, g)
+
+        def add_bias(key, column):
+            biased[key] = work.tile([P, PASS], F32, name="biased", bufs=3)
+            nc.scalar.activation(
+                out=biased[key][:], in_=logits[key][:], func=ACT.Identity, bias=bias[:, column : column + 1], scale=1.0
+            )
+
+        def word_bias(i):
+            u, q = divmod(i, BLOCKS)
+            add_bias(i, (u // N_GROUPS) * BLOCKS + q)
+
+        def turn_z(key, tag):
+            turned_z[key] = bank(tag, [P, PACK, P])
+            for t in range(PACK):
+                nc.tensor.transpose(turned_z[key][:, t, :], biased[key][:, t * P : (t + 1) * P], ident[:])
+
+        def word_max(i):
+            top[i] = work.tile([P, BLOCK_CLUSTERS, PACK], F32, name="top", bufs=3)
+            nc.vector.tensor_reduce(
+                out=top[i][:], in_=turned_z[i][:].rearrange("p t (c l) -> p c t l", l=L), axis=AXIS.X, op=ALU.max
+            )
+
+        def word_sub(i):
+            shifted[i] = work.tile([P, L, BLOCK_CLUSTERS, PACK], F32, name="shifted", bufs=3)
+            nc.vector.tensor_tensor(
+                out=shifted[i][:],
+                in0=turned_z[i][:].rearrange("p t (c l) -> p l c t", l=L),
+                in1=top[i][:].unsqueeze(1).broadcast_to([P, L, BLOCK_CLUSTERS, PACK]),
+                op=ALU.subtract,
+            )
+
+        def word_exp(i):
+            u, q = divmod(i, BLOCKS)
+            if q == 0:
+                expd[u] = work.tile([P, L, CHUNK_CLUSTERS * PACK], F32, name="expd", bufs=3)
+            w = BLOCK_CLUSTERS * PACK
+            nc.scalar.activation(
+                out=expd[u][:, :, q * w : (q + 1) * w],
+                in_=shifted[i][:].rearrange("p l c t -> p l (c t)"),
+                func=ACT.Exp,
+            )
+
+        sums = {}
+        inverse = {}
+        factor = {}
+        gate = {}
+        h_grouped = {}
+        h_mx = {}
+
+        def sum_words(u):
+            sums[u] = bank("sum", [P, 2, P])
+            for l in range(L):
+                nc.tensor.matmul(
+                    sums[u][:, 0, :], lhsT=expd[u][:, l, :], rhs=ident[:], start=(l == 0), stop=(l == L - 1), is_transpose=True
+                )
+
+        def invert_sums(u):
+            inverse[u] = work.tile([P, P], F32, name="inverse")
+            nc.vector.reciprocal(out=inverse[u][:], in_=sums[u][:, 0, :])
+
+        def turn_inverse(u):
+            nc.tensor.transpose(sums[u][:, 1, :], inverse[u][:], ident[:])
+
+        def make_factor(u):
+            n, g = divmod(u, N_GROUPS)
+            factor[u] = work.tile([P, P], F32, name="factor")
+            clusters = slice(n * CHUNK_CLUSTERS, (n + 1) * CHUNK_CLUSTERS)
+            nc.vector.tensor_tensor(
+                out=factor[u][:].rearrange("p (c t) -> p c t", t=PACK),
+                in0=sums[u][:, 1, :].rearrange("p (c t) -> p c t", t=PACK),
+                in1=gate[g][:, :, clusters].rearrange("p t c -> p c t"),
+                op=ALU.mult,
+            )
+
+        def make_h(u, engine, part=0, parts=1):
+            w = P // parts
+            h_grouped[u, part] = work.tile([P, L, w], BF16, name="h_grouped", bufs=3, align_bytes=64)
+            cols = slice(part * w, (part + 1) * w)
+            engine.tensor_tensor(
+                out=h_grouped[u, part][:],
+                in0=expd[u][:, :, cols],
+                in1=factor[u][:, cols].unsqueeze(1).broadcast_to([P, L, w]),
+                op=ALU.mult,
+            )
+
+        def quantize_h(u, part=0, parts=1):
+            h_mx[u, part] = mx_operand("h_%d_%d" % (u, part), CHUNK // parts)
+            quantize(h_mx[u, part], h_grouped[u, part][:].rearrange("p l w -> p (l w)"))
+
+        wc_mx = mx_operand("wc", N_PASSES * C)
+        wc_grouped = keep.tile([P, N_PASSES, C, PACK], BF16, name="wc_grouped", align_bytes=64)
+        gate_top = {}
+        gate_exp = {}
+        gate_sum = {}
+        gate_inv = {}
+        gate_scale = {}
+
+        def gate_max(g):
+            gate_top[g] = keep.tile([P, PACK], F32, name="gate_top_%d" % g)
+            nc.vector.tensor_reduce(out=gate_top[g][:], in_=turned_z["c", g][:], axis=AXIS.X, op=ALU.max, negate=True)
+
+        def gate_exps(g):
+            gate_exp[g] = keep.tile([P, PACK, C], F32, name="gate_exp_%d" % g)
+            gate_sum[g] = keep.tile([P, PACK], F32, name="gate_sum_%d" % g)
+            for t in range(PACK):
+                nc.scalar.activation(
+                    out=gate_exp[g][:, t, :],
+                    in_=turned_z["c", g][:, t, :],
+                    func=ACT.Exp,
+                    bias=gate_top[g][:, t : t + 1],
+                    scale=1.0,
+                    accum_out=gate_sum[g][:, t : t + 1],
+                )
+
+        def gate_invert(g):
+            gate_inv[g] = keep.tile([P, PACK], F32, name="gate_inv_%d" % g)
+            nc.vector.reciprocal(out=gate_inv[g][:], in_=gate_sum[g][:])
+
+        def gate_weigh(g):
+            gate_scale[g] = keep.tile([P, PACK], F32, name="gate_scale_%d" % g)
+            nc.vector.scalar_tensor_tensor(
+                out=gate_scale[g][:], in0=gate_inv[g][:], scalar=float(C * L), in1=imp[:, g, :], op0=ALU.mult, op1=ALU.mult
+            )
+
+        def gate_finish(g):
+            gate[g] = keep.tile([P, PACK, C], F32, name="gate_%d" % g)
+            for t in range(PACK):
+                nc.scalar.activation(
+                    out=gate[g][:, t, :], in_=gate_exp[g][:, t, :], func=ACT.Copy, scale=gate_scale[g][:, t : t + 1]
+                )
+
+        pool_grouped = keep.tile([P, N_GROUPS, J, 2], F32, name="pool_grouped", align_bytes=64)
+        pool_mx = mx_operand("pool", N_GROUPS * J)
+
+        def turn_pool(jt):
+            words = pool_raw[:].bitcast(F32)
+            turned = bank("out", [P, N_GROUPS, 2, P])
+            for g in range(N_GROUPS):
+                for u in range(2):
+                    nc.tensor.transpose(turned[:, g, u, :], words[:, jt, 256 * g + u : 256 * (g + 1) : 2], ident[:])
+            nc.scalar.copy(out=pool_grouped[:, :, jt * P : (jt + 1) * P, :], in_=turned[:].rearrange("p g u r -> p g r u"))
+
+        pooled = {}
+
+        def pooled_mx(n, jt, tag, part=0, parts=1):
+            w = CHUNK // parts
+            acc = bank(tag, [P, w])
+            pooled[n, jt, part] = acc
+            for g in range(N_GROUPS):
+                mx_pass(acc[:], pool_mx, g * J + jt * P, h_mx[N_GROUPS * n + g, part], 0, w, g == 0, g == N_GROUPS - 1)
+
+        def store(n, jt, part=0, parts=1):
+            w = CHUNK // parts
+            cols = slice(n * CHUNK + part * w, n * CHUNK + (part + 1) * w)
+            result = work.tile([P, w], F32, name="result", bufs=8)
+            nc.vector.tensor_tensor(
+                out=result[:].rearrange("p (c l) -> p c l", l=L),
+                in0=pooled[n, jt, part][:].rearrange("p (l c) -> p c l", l=L),
+                in1=idf_rows[:, cols].rearrange("p (c l) -> p c l", l=L),
+                op=ALU.mult,
+            )
+            nc.sync.dma_start(out=out[jt * P : (jt + 1) * P, cols], in_=result[:])
+
+        warm = keep.tile([P, 1], F32, name="warm")
+        nc.scalar.activation(out=warm[:], in_=ident[:, 0:1], func=ACT.Exp)
+        turn_x(0, 0, ("out", "out"), ("scalar", "scalar"))
+        interleave_w(0, 0, 0, PIECE, "vector")
+        turned_bias = bank("sum", [P, P], BF16)
+        nc.tensor.transpose(turned_bias[:], bias_rows[:], ident_bf[:])
+        nc.scalar.copy(out=bias[:], in_=turned_bias[:, 0:32])
+        quantize_x(0, 0)
+        interleave_w(0, 1, 0, PIECE, "vector")
+        turn_x(0, 1, ("z", "z"), ("scalar", "vector"))
+        quantize_w(0)
+        quantize_x(0, 1)
+        interleave_w(1, 0, 0, PIECE, "scalar")
+        word_mx(0)
+        word_mx(1)
+        interleave_w(1, 1, 0, PIECE, "vector")
+        turn_x(1, 0, ("out", "out"), ("vector", "vector"))
+        word_bias(0)
+        word_bias(1)
+        turn_z(0, "z")
+        quantize_w(1)
+
+        pool_steps = {6: 0, 7: 1, 12: 2, 13: 3}
+        for s in range(N_TILES + 1):
+            u, slot = divmod(s, BLOCKS)
+            piece = u + 2
+            if s + 2 < N_TILES:
+                word_mx(s + 2)
+                word_bias(s + 2)
+            if s in (3, 7):
+                logits_mx(("c", s // 4), wc_mx, 0, C, s // 4)
+            if s >= 16 and s % 2 == 0:
+                pooled_mx((s - 16) // 8, (s % 8) // 2, "out")
+            if s + 1 < N_TILES:
+                turn_z(s + 1, "z")
+            if slot == 3 and u >= 1:
+                turn_inverse(u - 1)
+            if slot == 1 and u >= 1:
+                sum_words(u - 1)
+            if s == 0:
+                turn_x(1, 1, ("out", "out"), ("scalar", "scalar"))
+            if s in (4, 8):
+                turn_z(("c", s // 4 - 1), "out")
+            if s < N_TILES:
+                word_max(s)
+            if s >= 1:
+                word_sub(s - 1)
+            ahead, part = divmod(s + 1, BLOCKS)
+            if s == 0:
+                interleave_w(2, 0, 0, P, "vector")
+            if ahead + 2 < 2 * N_CHUNKS:
+                interleave_w(ahead + 2, part % 2, (part // 2) * P, P, "scalar" if s > 6 else "vector")
+            if s >= 1:
+                word_exp(s - 1)
+            if s == 1:
+                for k in range(N_PASSES):
+                    interleave("scalar", wc_grouped[:, k, :, :], wc_raw[:, k, :, :])
+            if s in (3, 7):
+                add_bias(("c", s // 4), V // P)
+            if s in pool_steps:
+                turn_pool(pool_steps[s])
+            if s in (0, 1):
+                quantize_x(1, s)
+            if s == 2:
+                quantize(wc_mx, wc_grouped[:].rearrange("p k c j -> p (k c j)"))
+            if s in (4, 8):
+                gate_max(s // 4 - 1)
+            if s in (5, 9):
+                gate_exps(s // 4 - 1)
+            if s >= 17 and slot in (0, 1):
+                done = s - 16 - (2 if slot == 0 else 1)
+                store(done // 8, (done % 8) // 2)
+            if s in (6, 10):
+                gate_invert(s // 4 - 1)
+            if slot == 2 and u >= 1:
+                invert_sums(u - 1)
+            if s in (6, 10):
+                gate_weigh(s // 4 - 1)
+                gate_finish(s // 4 - 1)
+            if slot == 3:
+                if piece < 2 * N_CHUNKS:
+                    quantize_w(piece)
+                if s == 15:
+                    quantize(pool_mx, pool_grouped[:].rearrange("p g j u -> p (g j u)").bitcast(BF16))
+                if u >= 2:
+                    quantize_h(u - 2)
+                if u >= 1:
+                    make_factor(u - 1)
+                    parts = 2 if u == N_UNITS - 1 else 1
+                    for part in range(parts):
+                        make_h(u - 1, nc.gpsimd, part, parts)
+
+        last = N_UNITS - 1
+        pooled_mx(2, 1, "mx")
+        pooled_mx(2, 2, "mx")
+        pooled_mx(2, 3, "z")
+        sum_words(last)
+        for jt in range(J_TILES):
+            store(2, jt)
+        invert_sums(last)
+        turn_inverse(last)
+        quantize_h(last - 1, 0, 2)
+        make_factor(last)
+        quantize_h(last - 1, 1, 2)
+        make_h(last, nc.vector, 0, 2)
+        make_h(last, nc.vector, 1, 2)
+        quantize_h(last, 0, 2)
+        quantize_h(last, 1, 2)
+        for jt in range(J_TILES):
+            pooled_mx(3, jt, ("out", "out", "mx", "mx")[jt], 0, 2)
+        for jt in range(J_TILES):
+            store(3, jt, 0, 2)
+            pooled_mx(3, jt, ("z", "z", "z", "out")[jt], 1, 2)
+        for jt in range(J_TILES):
+            store(3, jt, 1, 2)

@@ -116,6 +116,7 @@ def tile_hierarchical_softmax_pooling_f4_kernel(
 
         x_mx = {}
         x_grouped = {}
+        x_turned = {}
 
         def copy_on(engine, dst, src):
             if engine == "vector":
@@ -123,16 +124,18 @@ def tile_hierarchical_softmax_pooling_f4_kernel(
             else:
                 nc.scalar.copy(out=dst, in_=src)
 
-        def turn_x(g, k, tags, engines):
-            grouped = work.tile([P, PACK, P, 2], F32, name="x_grouped", align_bytes=64)
-            x_grouped[g, k] = grouped
+        def turn_x(g, k, tags):
             words = x_raw[g, k][:].bitcast(F32)
             for half in range(2):
-                turned = bank(tags[half], [P, 2, 2, P])
+                x_turned[g, k, half] = bank(tags[half], [P, 2, 2, P])
                 for t in range(2):
                     for u in range(2):
-                        nc.tensor.transpose(turned[:, t, u, :], words[:, 2 * half + t, u::2], ident[:])
-                copy_on(engines[half], grouped[:, 2 * half : 2 * half + 2, :, :], turned[:].rearrange("p t u r -> p t r u"))
+                        nc.tensor.transpose(x_turned[g, k, half][:, t, u, :], words[:, 2 * half + t, u::2], ident[:])
+
+        def group_x(g, k, half, engine):
+            if half == 0:
+                x_grouped[g, k] = work.tile([P, PACK, P, 2], F32, name="x_grouped", align_bytes=64)
+            copy_on(engine, x_grouped[g, k][:, 2 * half : 2 * half + 2, :, :], x_turned[g, k, half][:].rearrange("p t u r -> p t r u"))
 
         def quantize_x(g, k):
             x_mx[g, k] = mx_operand("x_%d_%d" % (g, k), PASS)
@@ -146,7 +149,7 @@ def tile_hierarchical_softmax_pooling_f4_kernel(
 
         def interleave_w(piece, k, c0, width, engine):
             if piece not in w_grouped:
-                w_grouped[piece] = work.tile([P, N_PASSES, PIECE, PACK], BF16, name="w_grouped", align_bytes=64)
+                w_grouped[piece] = work.tile([P, N_PASSES, PIECE, PACK], BF16, name="w_grouped", bufs=3, align_bytes=64)
             interleave(engine, w_grouped[piece][:, k, c0 : c0 + width, :], w_raw[k, piece][:, :, c0 : c0 + width])
 
         def quantize_w(piece):
@@ -181,10 +184,17 @@ def tile_hierarchical_softmax_pooling_f4_kernel(
             u, q = divmod(i, BLOCKS)
             add_bias(i, (u // N_GROUPS) * BLOCKS + q)
 
-        def turn_z(key, tag):
+        def turn_z(key, tag, plain=0):
             turned_z[key] = bank(tag, [P, PACK, P])
             for t in range(PACK):
-                nc.tensor.transpose(turned_z[key][:, t, :], biased[key][:, t * P : (t + 1) * P], ident[:])
+                nc.tensor.matmul(
+                    turned_z[key][:, t, :],
+                    lhsT=biased[key][:, t * P : (t + 1) * P],
+                    rhs=ident[:],
+                    start=True,
+                    stop=True,
+                    is_transpose=(t < PACK - plain),
+                )
 
         def word_max(i):
             top[i] = work.tile([P, BLOCK_CLUSTERS, PACK], F32, name="top", bufs=3)
@@ -204,7 +214,7 @@ def tile_hierarchical_softmax_pooling_f4_kernel(
         def word_exp(i):
             u, q = divmod(i, BLOCKS)
             if q == 0:
-                expd[u] = work.tile([P, L, CHUNK_CLUSTERS * PACK], F32, name="expd", bufs=3)
+                expd[u] = work.tile([P, L, CHUNK_CLUSTERS * PACK], F32, name="expd", bufs=4)
             w = BLOCK_CLUSTERS * PACK
             nc.scalar.activation(
                 out=expd[u][:, :, q * w : (q + 1) * w],
@@ -219,19 +229,29 @@ def tile_hierarchical_softmax_pooling_f4_kernel(
         h_grouped = {}
         h_mx = {}
 
-        def sum_words(u):
-            sums[u] = bank("sum", [P, 2, P])
-            for l in range(L):
+        def sum_words(u, words, plain):
+            if words[0] == 0:
+                sums[u] = bank("sum", [P, 2, P])
+            for l in words:
                 nc.tensor.matmul(
-                    sums[u][:, 0, :], lhsT=expd[u][:, l, :], rhs=ident[:], start=(l == 0), stop=(l == L - 1), is_transpose=True
+                    sums[u][:, 0, :],
+                    lhsT=expd[u][:, l, :],
+                    rhs=ident[:],
+                    start=(l == 0),
+                    stop=(l == L - 1),
+                    is_transpose=l not in plain,
                 )
 
         def invert_sums(u):
             inverse[u] = work.tile([P, P], F32, name="inverse")
             nc.vector.reciprocal(out=inverse[u][:], in_=sums[u][:, 0, :])
 
-        def turn_inverse(u):
-            nc.tensor.transpose(sums[u][:, 1, :], inverse[u][:], ident[:])
+        def turn_inverse(u, plain):
+            nc.tensor.matmul(sums[u][:, 1, :], lhsT=inverse[u][:], rhs=ident[:], start=True, stop=True, is_transpose=not plain)
+
+        def keep_warm(tag, blocks):
+            idle = bank(tag, [P, blocks, P])
+            nc.tensor.matmul(idle[:], lhsT=ident[:], rhs=ident[:].unsqueeze(1).broadcast_to([P, blocks, P]), start=True, stop=True)
 
         def make_factor(u):
             n, g = divmod(u, N_GROUPS)
@@ -304,13 +324,18 @@ def tile_hierarchical_softmax_pooling_f4_kernel(
         pool_grouped = keep.tile([P, N_GROUPS, J, 2], F32, name="pool_grouped", align_bytes=64)
         pool_mx = mx_operand("pool", N_GROUPS * J)
 
+        pool_turned = {}
+
         def turn_pool(jt):
             words = pool_raw[:].bitcast(F32)
             turned = bank("out", [P, N_GROUPS, 2, P])
+            pool_turned[jt] = turned
             for g in range(N_GROUPS):
                 for u in range(2):
                     nc.tensor.transpose(turned[:, g, u, :], words[:, jt, 256 * g + u : 256 * (g + 1) : 2], ident[:])
-            nc.scalar.copy(out=pool_grouped[:, :, jt * P : (jt + 1) * P, :], in_=turned[:].rearrange("p g u r -> p g r u"))
+
+        def group_pool(jt, engine):
+            copy_on(engine, pool_grouped[:, :, jt * P : (jt + 1) * P, :], pool_turned[jt][:].rearrange("p g u r -> p g r u"))
 
         pooled = {}
 
@@ -320,6 +345,12 @@ def tile_hierarchical_softmax_pooling_f4_kernel(
             pooled[n, jt, part] = acc
             for g in range(N_GROUPS):
                 mx_pass(acc[:], pool_mx, g * J + jt * P, h_mx[N_GROUPS * n + g, part], 0, w, g == 0, g == N_GROUPS - 1)
+
+        def pooled_pass(n, jt, g, tag="out", part=0, parts=1):
+            w = CHUNK // parts
+            if g == 0:
+                pooled[n, jt, part] = bank(tag, [P, w])
+            mx_pass(pooled[n, jt, part][:], pool_mx, g * J + jt * P, h_mx[N_GROUPS * n + g, part], 0, w, g == 0, g == N_GROUPS - 1)
 
         def store(n, jt, part=0, parts=1):
             w = CHUNK // parts
@@ -335,116 +366,152 @@ def tile_hierarchical_softmax_pooling_f4_kernel(
 
         warm = keep.tile([P, 1], F32, name="warm")
         nc.scalar.activation(out=warm[:], in_=ident[:, 0:1], func=ACT.Exp)
-        turn_x(0, 0, ("out", "out"), ("scalar", "scalar"))
+        turn_x(0, 0, ("out", "out"))
+        group_x(0, 0, 0, "scalar")
+        group_x(0, 0, 1, "scalar")
         interleave_w(0, 0, 0, PIECE, "vector")
         turned_bias = bank("sum", [P, P], BF16)
         nc.tensor.transpose(turned_bias[:], bias_rows[:], ident_bf[:])
         nc.scalar.copy(out=bias[:], in_=turned_bias[:, 0:32])
         quantize_x(0, 0)
         interleave_w(0, 1, 0, PIECE, "vector")
-        turn_x(0, 1, ("z", "z"), ("scalar", "vector"))
+        turn_x(0, 1, ("z", "z"))
+        group_x(0, 1, 0, "scalar")
+        group_x(0, 1, 1, "vector")
         quantize_w(0)
         quantize_x(0, 1)
         interleave_w(1, 0, 0, PIECE, "scalar")
         word_mx(0)
         word_mx(1)
         interleave_w(1, 1, 0, PIECE, "vector")
-        turn_x(1, 0, ("out", "out"), ("vector", "vector"))
         word_bias(0)
         word_bias(1)
-        turn_z(0, "z")
         quantize_w(1)
+        turn_z(0, "z", 0)
+        turn_x(1, 0, ("out", "out"))
 
-        pool_steps = {6: 0, 7: 1, 12: 2, 13: 3}
+        first_pooled = 20
+        late = N_TILES - 4
         for s in range(N_TILES + 1):
             u, slot = divmod(s, BLOCKS)
-            piece = u + 2
+            gate_g, gate_step = divmod(s - 3, BLOCKS)
+            gate_at = {g: s - 3 - BLOCKS * g for g in range(N_GROUPS)}
             if s + 2 < N_TILES:
                 word_mx(s + 2)
-                word_bias(s + 2)
-            if s in (3, 7):
-                logits_mx(("c", s // 4), wc_mx, 0, C, s // 4)
-            if s >= 16 and s % 2 == 0:
-                pooled_mx((s - 16) // 8, (s % 8) // 2, "out")
+            for g in range(N_GROUPS):
+                if gate_at[g] == 0:
+                    logits_mx(("c", g), wc_mx, 0, C, g)
+            if first_pooled <= s < late and slot in (0, 1):
+                pooled_mx(0, (s - first_pooled) // 2 + slot, "out")
+            if late <= s < N_TILES:
+                pooled_mx(1, s - late, "out")
             if s + 1 < N_TILES:
-                turn_z(s + 1, "z")
-            if slot == 3 and u >= 1:
-                turn_inverse(u - 1)
-            if slot == 1 and u >= 1:
-                sum_words(u - 1)
-            if s == 0:
-                turn_x(1, 1, ("out", "out"), ("scalar", "scalar"))
-            if s in (4, 8):
-                turn_z(("c", s // 4 - 1), "out")
+                turn_z(s + 1, "z", 1 if s < 20 else 0)
+            if (slot == 1 and u >= 2) or s == N_TILES:
+                turn_inverse(u - 2, False)
+            if slot in (2, 3) and 1 <= u < N_UNITS - 1:
+                sum_words(u - 1, range((slot - 2) * L // 2, (slot - 1) * L // 2), ())
+            if s == N_TILES - 2:
+                sum_words(u - 1, range(L), ())
+            for g in range(N_GROUPS):
+                if gate_at[g] == 1:
+                    turn_z(("c", g), "out")
+            if 12 <= s < 12 + J_TILES:
+                turn_pool(s - 12)
             if s < N_TILES:
                 word_max(s)
             if s >= 1:
                 word_sub(s - 1)
-            ahead, part = divmod(s + 1, BLOCKS)
-            if s == 0:
-                interleave_w(2, 0, 0, P, "vector")
-            if ahead + 2 < 2 * N_CHUNKS:
-                interleave_w(ahead + 2, part % 2, (part // 2) * P, P, "scalar" if s > 6 else "vector")
-            if s >= 1:
+            if 2 <= s <= late:
+                word_exp(s - 2)
+            if s >= late:
                 word_exp(s - 1)
+            if s + 2 < N_TILES:
+                word_bias(s + 2)
+            piece, part = divmod(s + 11, BLOCKS)
+            if 4 <= piece < 2 * N_CHUNKS:
+                interleave_w(piece, part % 2, (part // 2) * P, P, "scalar")
             if s == 1:
                 for k in range(N_PASSES):
                     interleave("scalar", wc_grouped[:, k, :, :], wc_raw[:, k, :, :])
-            if s in (3, 7):
-                add_bias(("c", s // 4), V // P)
-            if s in pool_steps:
-                turn_pool(pool_steps[s])
-            if s in (0, 1):
-                quantize_x(1, s)
+            for g in range(N_GROUPS):
+                if gate_at[g] == 0:
+                    add_bias(("c", g), V // P)
+                if gate_at[g] == 3:
+                    gate_exps(g)
+                if gate_at[g] == 5:
+                    gate_finish(g)
+            if s == 0:
+                group_x(1, 0, 0, "vector")
+                group_x(1, 0, 1, "vector")
+                turn_x(1, 1, ("out", "out"))
+                group_x(1, 1, 0, "scalar")
+                group_x(1, 1, 1, "scalar")
+            if s == 1:
+                quantize_x(1, 0)
+                quantize_x(1, 1)
             if s == 2:
                 quantize(wc_mx, wc_grouped[:].rearrange("p k c j -> p (k c j)"))
-            if s in (4, 8):
-                gate_max(s // 4 - 1)
-            if s in (5, 9):
-                gate_exps(s // 4 - 1)
-            if s >= 17 and slot in (0, 1):
-                done = s - 16 - (2 if slot == 0 else 1)
-                store(done // 8, (done % 8) // 2)
-            if s in (6, 10):
-                gate_invert(s // 4 - 1)
-            if slot == 2 and u >= 1:
+            if 2 <= s < 6:
+                interleave_w(2 + (s - 2) // 2, s % 2, 0, PIECE, "vector")
+            if s in (4, 6):
+                quantize_w(s // 2)
+            for g in range(N_GROUPS):
+                if gate_at[g] == 2:
+                    gate_max(g)
+                if gate_at[g] == 4:
+                    gate_invert(g)
+            if 12 < s <= 12 + J_TILES:
+                group_pool(s - 1 - 12, "scalar")
+            if first_pooled <= s < late and slot in (2, 3):
+                store(0, (s - first_pooled - 2) // 2 + slot - 2)
+            if late < s < N_TILES:
+                store(1, s - late - 1)
+            if slot == 0 and 2 <= u < N_UNITS:
+                invert_sums(u - 2)
+            if s == N_TILES - 1:
                 invert_sums(u - 1)
-            if s in (6, 10):
-                gate_weigh(s // 4 - 1)
-                gate_finish(s // 4 - 1)
-            if slot == 3:
-                if piece < 2 * N_CHUNKS:
-                    quantize_w(piece)
-                if s == 15:
-                    quantize(pool_mx, pool_grouped[:].rearrange("p g j u -> p (g j u)").bitcast(BF16))
-                if u >= 2:
-                    quantize_h(u - 2)
-                if u >= 1:
-                    make_factor(u - 1)
-                    parts = 2 if u == N_UNITS - 1 else 1
-                    for part in range(parts):
-                        make_h(u - 1, nc.gpsimd, part, parts)
+            for g in range(N_GROUPS):
+                if gate_at[g] == 4:
+                    gate_weigh(g)
+            if slot == 1 and 4 <= u + 2 < 2 * N_CHUNKS:
+                quantize_w(u + 2)
+            if s == 17:
+                quantize(pool_mx, pool_grouped[:].rearrange("p g j u -> p (g j u)").bitcast(BF16))
+            if (slot == 1 and u >= 2) or s == N_TILES:
+                if u >= 3:
+                    quantize_h(u - 3)
+                make_factor(u - 2)
+                parts = 2 if s == N_TILES else 1
+                for half in range(parts):
+                    make_h(u - 2, nc.gpsimd, half, parts)
 
         last = N_UNITS - 1
+        pooled_mx(2, 0, "out")
         pooled_mx(2, 1, "mx")
+        sum_words(last, range(L // 2), ())
         pooled_mx(2, 2, "mx")
+        sum_words(last, range(L // 2, L), ())
         pooled_mx(2, 3, "z")
-        sum_words(last)
-        for jt in range(J_TILES):
+        store(1, J_TILES - 1)
+        for jt in range(J_TILES - 1):
             store(2, jt)
         invert_sums(last)
-        turn_inverse(last)
-        quantize_h(last - 1, 0, 2)
+        turn_inverse(last, False)
+        store(2, J_TILES - 1)
         make_factor(last)
+        quantize_h(last - 1, 0, 2)
         quantize_h(last - 1, 1, 2)
+        tags = (("out", "out", "mx", "mx"), ("z", "z", "z", "sum"))
+        for half in range(2):
+            for jt in range(J_TILES):
+                pooled_pass(3, jt, 0, tags[half][jt], half, 2)
         make_h(last, nc.vector, 0, 2)
         make_h(last, nc.vector, 1, 2)
-        quantize_h(last, 0, 2)
-        quantize_h(last, 1, 2)
-        for jt in range(J_TILES):
-            pooled_mx(3, jt, ("out", "out", "mx", "mx")[jt], 0, 2)
-        for jt in range(J_TILES):
-            store(3, jt, 0, 2)
-            pooled_mx(3, jt, ("z", "z", "z", "out")[jt], 1, 2)
-        for jt in range(J_TILES):
-            store(3, jt, 1, 2)
+        for half in range(2):
+            quantize_h(last, half, 2)
+            for jt in range(J_TILES):
+                pooled_pass(3, jt, 1, tags[half][jt], half, 2)
+        for half in range(2):
+            for jt in range(J_TILES):
+                store(3, jt, half, 2)

@@ -18,17 +18,20 @@ AXIS = mybir.AxisListType
 P = 128
 PACK = 4
 PASS = P * PACK
+N_PASSES = D // PASS
+N_GROUPS = T // PASS
 CHUNK = 512
 N_CHUNKS = V // CHUNK
-N_GROUPS = T // PASS
-N_PASSES = D // PASS
-BLOCKS = CHUNK // P
+TILES = CHUNK // P
 N_UNITS = N_CHUNKS * N_GROUPS
-N_TILES = N_UNITS * BLOCKS
+N_TILES = N_UNITS * TILES
 CHUNK_CLUSTERS = CHUNK // L
-BLOCK_CLUSTERS = P // L
+TILE_CLUSTERS = P // L
 PIECE = CHUNK // 2
+N_PIECES = V // PIECE
 J_TILES = J // P
+CLUSTER_BIAS = V // P
+BANKS = {"mx": 2, "z": 3, "sum": 1, "out": 2}
 
 
 def tile_hierarchical_softmax_pooling_f4_kernel(
@@ -41,29 +44,35 @@ def tile_hierarchical_softmax_pooling_f4_kernel(
         psum = ctx.enter_context(tc.psum_pool(name="psum", bufs=1))
         ctx.enter_context(tc.manual_schedule())
 
-        def bank(tag, shape, dtype=F32):
-            depth = {"mx": 2, "z": 3, "sum": 1, "out": 2}[tag]
-            return psum.tile(shape, dtype, name="bank_" + tag, tag=tag, bufs=depth)
+        def bank(role, shape, dtype=F32):
+            return psum.tile(shape, dtype, name="bank_" + role, tag=role, bufs=BANKS[role])
 
-        def mx_operand(name, columns):
+        def quantize(name, grouped):
+            columns = grouped.shape[1] // PACK
             codes = keep.tile([P, columns], U32, name=name + "_codes", align_bytes=64)
             scales = keep.tile([P, columns], U8, name=name + "_scales", align_bytes=64)
+            nc.vector.quantize_mx(out=codes[:].bitcast(FP8X4), scales=scales[:], in_=grouped)
             return codes, scales
 
-        def quantize(operand, grouped):
-            codes, scales = operand
-            nc.vector.quantize_mx(out=codes[:].bitcast(FP8X4), scales=scales[:], in_=grouped)
-
-        def mx_pass(acc, stationary, m0, moving, n0, width, first, last):
+        def mx_pass(acc, stationary, m0, moving, first, last):
             nc.tensor.matmul_mx(
                 out=acc,
                 lhsT=stationary[0][:, m0 : m0 + P].bitcast(FP8X4),
                 lhsT_scale=stationary[1][:, m0 : m0 + P],
-                rhs=moving[0][:, n0 : n0 + width].bitcast(FP8X4),
-                rhs_scale=moving[1][:, n0 : n0 + width],
+                rhs=moving[0][:].bitcast(FP8X4),
+                rhs_scale=moving[1][:],
                 start=first,
                 stop=last,
             )
+
+        def copy_on(engine, dst, src):
+            if engine == "vector":
+                nc.vector.tensor_copy(out=dst, in_=src)
+            else:
+                nc.scalar.copy(out=dst, in_=src)
+
+        def interleave(engine, dst, src):
+            copy_on(engine, dst.rearrange("p (c i) j -> p c j i", i=4), src.rearrange("p j (c i) -> p c j i", i=4))
 
         bias_rows = keep.tile([P, P], BF16, name="bias_rows")
         nc.gpsimd.memset(bias_rows[:], 0.0)
@@ -80,20 +89,20 @@ def tile_hierarchical_softmax_pooling_f4_kernel(
             rows = x[g * PASS : (g + 1) * PASS, k * PASS : (k + 1) * PASS]
             nc.sync.dma_start(out=x_raw[g, k][:], in_=rows.rearrange("(p t) d -> p t d", t=PACK))
 
-        def load_w(k, v0, width):
-            raw = keep.tile([P, PACK, width], BF16, name="w_raw_%d_%d" % (k, v0))
-            rows = w_word[k * PASS : (k + 1) * PASS, v0 : v0 + width]
+        def load_w(k, first_piece, pieces):
+            raw = keep.tile([P, PACK, pieces * PIECE], BF16, name="w_raw_%d_%d" % (k, first_piece))
+            rows = w_word[k * PASS : (k + 1) * PASS, first_piece * PIECE : (first_piece + pieces) * PIECE]
             nc.sync.dma_start(out=raw[:], in_=rows.rearrange("(p j) v -> p j v", j=PACK))
-            for c0 in range(0, width, PIECE):
-                w_raw[k, (v0 + c0) // PIECE] = raw[:, :, c0 : c0 + PIECE]
+            for r in range(pieces):
+                w_raw[k, first_piece + r] = raw[:, :, r * PIECE : (r + 1) * PIECE]
 
         for k in range(N_PASSES):
             load_x(0, k)
-            load_w(k, 0, PIECE)
-        nc.scalar.dma_start(out=bias_rows[0 : V // P, :], in_=b_word.rearrange("(q p) -> q p", p=P))
-        nc.scalar.dma_start(out=bias_rows[V // P : V // P + 1, :], in_=b_cluster.rearrange("(q p) -> q p", p=P))
+            load_w(k, 0, 1)
+        nc.scalar.dma_start(out=bias_rows[0:CLUSTER_BIAS, :], in_=b_word.rearrange("(q p) -> q p", p=P))
+        nc.scalar.dma_start(out=bias_rows[CLUSTER_BIAS : CLUSTER_BIAS + 1, :], in_=b_cluster.rearrange("(q p) -> q p", p=P))
         for k in range(N_PASSES):
-            load_w(k, PIECE, PIECE)
+            load_w(k, 1, 1)
         for k in range(N_PASSES):
             load_x(1, k)
         wc_raw = keep.tile([P, N_PASSES, PACK, C], BF16, name="wc_raw")
@@ -102,61 +111,54 @@ def tile_hierarchical_softmax_pooling_f4_kernel(
             in_=w_cluster.rearrange("(k p j) c -> p k (j c)", p=P, j=PACK),
         )
         for k in range(N_PASSES):
-            load_w(k, CHUNK, CHUNK)
+            load_w(k, 2, 2)
         imp = keep.tile([P, N_GROUPS, PACK], BF16, name="imp")
         nc.sync.dma_start(out=imp[:], in_=importance.rearrange("(g p t) -> p g t", p=P, t=PACK))
         pool_raw = keep.tile([P, J_TILES, T], BF16, name="pool_raw")
         nc.sync.dma_start(out=pool_raw[:], in_=pool.rearrange("(jt j) t -> j jt t", j=P))
         for k in range(N_PASSES):
-            load_w(k, 2 * CHUNK, CHUNK)
+            load_w(k, 4, 2)
         idf_rows = keep.tile([P, V], BF16, name="idf_rows")
         nc.sync.dma_start(out=idf_rows[:], in_=idf.partition_broadcast(P))
         for k in range(N_PASSES):
-            load_w(k, 3 * CHUNK, CHUNK)
+            load_w(k, 6, 2)
 
-        x_mx = {}
-        x_grouped = {}
         x_turned = {}
+        x_grouped = {}
+        x_mx = {}
 
-        def copy_on(engine, dst, src):
-            if engine == "vector":
-                nc.vector.tensor_copy(out=dst, in_=src)
-            else:
-                nc.scalar.copy(out=dst, in_=src)
-
-        def turn_x(g, k, tags):
+        def turn_x(g, k, role):
             words = x_raw[g, k][:].bitcast(F32)
             for half in range(2):
-                x_turned[g, k, half] = bank(tags[half], [P, 2, 2, P])
+                x_turned[g, k, half] = bank(role, [P, 2, 2, P])
                 for t in range(2):
                     for u in range(2):
                         nc.tensor.transpose(x_turned[g, k, half][:, t, u, :], words[:, 2 * half + t, u::2], ident[:])
 
-        def group_x(g, k, half, engine):
-            if half == 0:
-                x_grouped[g, k] = work.tile([P, PACK, P, 2], F32, name="x_grouped", align_bytes=64)
-            copy_on(engine, x_grouped[g, k][:, 2 * half : 2 * half + 2, :, :], x_turned[g, k, half][:].rearrange("p t u r -> p t r u"))
+        def group_x(g, k, engines):
+            x_grouped[g, k] = work.tile([P, PACK, P, 2], F32, name="x_grouped", align_bytes=64)
+            for half in range(2):
+                copy_on(
+                    engines[half],
+                    x_grouped[g, k][:, 2 * half : 2 * half + 2, :, :],
+                    x_turned[g, k, half][:].rearrange("p t u r -> p t r u"),
+                )
 
         def quantize_x(g, k):
-            x_mx[g, k] = mx_operand("x_%d_%d" % (g, k), PASS)
-            quantize(x_mx[g, k], x_grouped[g, k][:].rearrange("p t r u -> p (t r u)").bitcast(BF16))
+            x_mx[g, k] = quantize("x_%d_%d" % (g, k), x_grouped[g, k][:].rearrange("p t r u -> p (t r u)").bitcast(BF16))
 
         w_grouped = {}
         w_mx = {}
 
-        def interleave(engine, dst, src):
-            copy_on(engine, dst.rearrange("p (c i) j -> p c j i", i=4), src.rearrange("p j (c i) -> p c j i", i=4))
-
-        def interleave_w(piece, k, c0, width, engine):
+        def interleave_w(piece, k, v0, width, engine):
             if piece not in w_grouped:
                 w_grouped[piece] = work.tile([P, N_PASSES, PIECE, PACK], BF16, name="w_grouped", bufs=3, align_bytes=64)
-            interleave(engine, w_grouped[piece][:, k, c0 : c0 + width, :], w_raw[k, piece][:, :, c0 : c0 + width])
+            interleave(engine, w_grouped[piece][:, k, v0 : v0 + width, :], w_raw[k, piece][:, :, v0 : v0 + width])
 
         def quantize_w(piece):
-            w_mx[piece] = mx_operand("w_%d" % piece, N_PASSES * PIECE)
-            quantize(w_mx[piece], w_grouped[piece][:].rearrange("p k v j -> p (k v j)"))
+            w_mx[piece] = quantize("w_%d" % piece, w_grouped[piece][:].rearrange("p k v j -> p (k v j)"))
 
-        bias = keep.tile([P, 32], F32, name="bias")
+        bias = keep.tile([P, CLUSTER_BIAS + 1], F32, name="bias")
         logits = {}
         biased = {}
         turned_z = {}
@@ -164,15 +166,10 @@ def tile_hierarchical_softmax_pooling_f4_kernel(
         shifted = {}
         expd = {}
 
-        def logits_mx(key, stationary, m0, m_step, g):
+        def logits_mx(key, stationary, m0, pass_columns, g):
             logits[key] = bank("mx", [P, PASS])
             for k in range(N_PASSES):
-                mx_pass(logits[key][:], stationary, m0 + k * m_step, x_mx[g, k], 0, PASS, k == 0, k == N_PASSES - 1)
-
-        def word_mx(i):
-            u, q = divmod(i, BLOCKS)
-            n, g = divmod(u, N_GROUPS)
-            logits_mx(i, w_mx[2 * n + q // 2], (q % 2) * P, PIECE, g)
+                mx_pass(logits[key][:], stationary, m0 + k * pass_columns, x_mx[g, k], k == 0, k == N_PASSES - 1)
 
         def add_bias(key, column):
             biased[key] = work.tile([P, PASS], F32, name="biased", bufs=3)
@@ -180,12 +177,8 @@ def tile_hierarchical_softmax_pooling_f4_kernel(
                 out=biased[key][:], in_=logits[key][:], func=ACT.Identity, bias=bias[:, column : column + 1], scale=1.0
             )
 
-        def word_bias(i):
-            u, q = divmod(i, BLOCKS)
-            add_bias(i, (u // N_GROUPS) * BLOCKS + q)
-
-        def turn_z(key, tag, plain=0):
-            turned_z[key] = bank(tag, [P, PACK, P])
+        def turn_z(key, role, products):
+            turned_z[key] = bank(role, [P, PACK, P])
             for t in range(PACK):
                 nc.tensor.matmul(
                     turned_z[key][:, t, :],
@@ -193,65 +186,69 @@ def tile_hierarchical_softmax_pooling_f4_kernel(
                     rhs=ident[:],
                     start=True,
                     stop=True,
-                    is_transpose=(t < PACK - plain),
+                    is_transpose=(t < PACK - products),
                 )
 
+        def word_mx(i):
+            u, q = divmod(i, TILES)
+            n, g = divmod(u, N_GROUPS)
+            logits_mx(i, w_mx[2 * n + q // 2], (q % 2) * P, PIECE, g)
+
+        def word_bias(i):
+            u, q = divmod(i, TILES)
+            add_bias(i, (u // N_GROUPS) * TILES + q)
+
         def word_max(i):
-            top[i] = work.tile([P, BLOCK_CLUSTERS, PACK], F32, name="top", bufs=3)
+            top[i] = work.tile([P, TILE_CLUSTERS, PACK], F32, name="top", bufs=3)
             nc.vector.tensor_reduce(
                 out=top[i][:], in_=turned_z[i][:].rearrange("p t (c l) -> p c t l", l=L), axis=AXIS.X, op=ALU.max
             )
 
         def word_sub(i):
-            shifted[i] = work.tile([P, L, BLOCK_CLUSTERS, PACK], F32, name="shifted", bufs=3)
+            shifted[i] = work.tile([P, L, TILE_CLUSTERS, PACK], F32, name="shifted", bufs=3)
             nc.vector.tensor_tensor(
                 out=shifted[i][:],
                 in0=turned_z[i][:].rearrange("p t (c l) -> p l c t", l=L),
-                in1=top[i][:].unsqueeze(1).broadcast_to([P, L, BLOCK_CLUSTERS, PACK]),
+                in1=top[i][:].unsqueeze(1).broadcast_to([P, L, TILE_CLUSTERS, PACK]),
                 op=ALU.subtract,
             )
 
         def word_exp(i):
-            u, q = divmod(i, BLOCKS)
+            u, q = divmod(i, TILES)
             if q == 0:
-                expd[u] = work.tile([P, L, CHUNK_CLUSTERS * PACK], F32, name="expd", bufs=4)
-            w = BLOCK_CLUSTERS * PACK
+                expd[u] = work.tile([P, L, P], F32, name="expd", bufs=4)
+            width = TILE_CLUSTERS * PACK
             nc.scalar.activation(
-                out=expd[u][:, :, q * w : (q + 1) * w],
+                out=expd[u][:, :, q * width : (q + 1) * width],
                 in_=shifted[i][:].rearrange("p l c t -> p l (c t)"),
                 func=ACT.Exp,
             )
 
         sums = {}
+        upper = {}
+        paired = {}
+        paired_inv = {}
         inverse = {}
         factor = {}
         gate = {}
         h_grouped = {}
         h_mx = {}
+        HALF = P // 2
 
-        def sum_words(u, words, plain):
+        def sum_words(u, words):
             if words[0] == 0:
                 sums[u] = bank("sum", [P, 2, P])
             for l in words:
                 nc.tensor.matmul(
-                    sums[u][:, 0, :],
-                    lhsT=expd[u][:, l, :],
-                    rhs=ident[:],
-                    start=(l == 0),
-                    stop=(l == L - 1),
-                    is_transpose=l not in plain,
+                    sums[u][:, 0, :], lhsT=expd[u][:, l, :], rhs=ident[:], start=(l == 0), stop=(l == L - 1), is_transpose=True
                 )
 
         def invert_sums(u):
             inverse[u] = work.tile([P, P], F32, name="inverse")
             nc.vector.reciprocal(out=inverse[u][:], in_=sums[u][:, 0, :])
 
-        def turn_inverse(u, plain):
-            nc.tensor.matmul(sums[u][:, 1, :], lhsT=inverse[u][:], rhs=ident[:], start=True, stop=True, is_transpose=not plain)
-
-        def keep_warm(tag, blocks):
-            idle = bank(tag, [P, blocks, P])
-            nc.tensor.matmul(idle[:], lhsT=ident[:], rhs=ident[:].unsqueeze(1).broadcast_to([P, blocks, P]), start=True, stop=True)
+        def turn_inverse(u):
+            nc.tensor.transpose(sums[u][:, 1, :], inverse[u][:], ident[:])
 
         def make_factor(u):
             n, g = divmod(u, N_GROUPS)
@@ -264,22 +261,20 @@ def tile_hierarchical_softmax_pooling_f4_kernel(
                 op=ALU.mult,
             )
 
-        def make_h(u, engine, part=0, parts=1):
-            w = P // parts
-            h_grouped[u, part] = work.tile([P, L, w], BF16, name="h_grouped", bufs=3, align_bytes=64)
-            cols = slice(part * w, (part + 1) * w)
+        def make_h(u, engine, part, parts):
+            width = P // parts
+            h_grouped[u, part] = work.tile([P, L, width], BF16, name="h_grouped", bufs=3, align_bytes=64)
+            cols = slice(part * width, (part + 1) * width)
             engine.tensor_tensor(
                 out=h_grouped[u, part][:],
                 in0=expd[u][:, :, cols],
-                in1=factor[u][:, cols].unsqueeze(1).broadcast_to([P, L, w]),
+                in1=factor[u][:, cols].unsqueeze(1).broadcast_to([P, L, width]),
                 op=ALU.mult,
             )
 
-        def quantize_h(u, part=0, parts=1):
-            h_mx[u, part] = mx_operand("h_%d_%d" % (u, part), CHUNK // parts)
-            quantize(h_mx[u, part], h_grouped[u, part][:].rearrange("p l w -> p (l w)"))
+        def quantize_h(u, part):
+            h_mx[u, part] = quantize("h_%d_%d" % (u, part), h_grouped[u, part][:].rearrange("p l w -> p (l w)"))
 
-        wc_mx = mx_operand("wc", N_PASSES * C)
         wc_grouped = keep.tile([P, N_PASSES, C, PACK], BF16, name="wc_grouped", align_bytes=64)
         gate_top = {}
         gate_exp = {}
@@ -310,9 +305,15 @@ def tile_hierarchical_softmax_pooling_f4_kernel(
 
         def gate_weigh(g):
             gate_scale[g] = keep.tile([P, PACK], F32, name="gate_scale_%d" % g)
-            nc.vector.scalar_tensor_tensor(
-                out=gate_scale[g][:], in0=gate_inv[g][:], scalar=float(C * L), in1=imp[:, g, :], op0=ALU.mult, op1=ALU.mult
-            )
+            for t in range(PACK):
+                nc.vector.tensor_scalar(
+                    out=gate_scale[g][:, t : t + 1],
+                    in0=gate_inv[g][:, t : t + 1],
+                    scalar1=imp[:, g, t : t + 1],
+                    scalar2=float(C * L),
+                    op0=ALU.mult,
+                    op1=ALU.mult,
+                )
 
         def gate_finish(g):
             gate[g] = keep.tile([P, PACK, C], F32, name="gate_%d" % g)
@@ -321,41 +322,37 @@ def tile_hierarchical_softmax_pooling_f4_kernel(
                     out=gate[g][:, t, :], in_=gate_exp[g][:, t, :], func=ACT.Copy, scale=gate_scale[g][:, t : t + 1]
                 )
 
-        pool_grouped = keep.tile([P, N_GROUPS, J, 2], F32, name="pool_grouped", align_bytes=64)
-        pool_mx = mx_operand("pool", N_GROUPS * J)
-
         pool_turned = {}
+        pool_grouped = keep.tile([P, N_GROUPS, J, 2], F32, name="pool_grouped", align_bytes=64)
 
         def turn_pool(jt):
-            words = pool_raw[:].bitcast(F32)
-            turned = bank("out", [P, N_GROUPS, 2, P])
-            pool_turned[jt] = turned
+            words = pool_raw[:].bitcast(F32).rearrange("j jt (g w) -> j jt g w", g=N_GROUPS)
+            pool_turned[jt] = bank("out", [P, N_GROUPS, 2, P])
             for g in range(N_GROUPS):
                 for u in range(2):
-                    nc.tensor.transpose(turned[:, g, u, :], words[:, jt, 256 * g + u : 256 * (g + 1) : 2], ident[:])
+                    nc.tensor.transpose(pool_turned[jt][:, g, u, :], words[:, jt, g, u::2], ident[:])
 
-        def group_pool(jt, engine):
-            copy_on(engine, pool_grouped[:, :, jt * P : (jt + 1) * P, :], pool_turned[jt][:].rearrange("p g u r -> p g r u"))
+        def group_pool(jt):
+            nc.scalar.copy(out=pool_grouped[:, :, jt * P : (jt + 1) * P, :], in_=pool_turned[jt][:].rearrange("p g u r -> p g r u"))
 
+        stage2 = {}
         pooled = {}
 
-        def pooled_mx(n, jt, tag, part=0, parts=1):
-            w = CHUNK // parts
-            acc = bank(tag, [P, w])
-            pooled[n, jt, part] = acc
-            for g in range(N_GROUPS):
-                mx_pass(acc[:], pool_mx, g * J + jt * P, h_mx[N_GROUPS * n + g, part], 0, w, g == 0, g == N_GROUPS - 1)
-
-        def pooled_pass(n, jt, g, tag="out", part=0, parts=1):
-            w = CHUNK // parts
+        def pooled_pass(n, jt, g, role, part, parts):
             if g == 0:
-                pooled[n, jt, part] = bank(tag, [P, w])
-            mx_pass(pooled[n, jt, part][:], pool_mx, g * J + jt * P, h_mx[N_GROUPS * n + g, part], 0, w, g == 0, g == N_GROUPS - 1)
+                pooled[n, jt, part] = bank(role, [P, CHUNK // parts])
+            mx_pass(
+                pooled[n, jt, part][:], stage2["pool"], g * J + jt * P, h_mx[N_GROUPS * n + g, part], g == 0, g == N_GROUPS - 1
+            )
 
-        def store(n, jt, part=0, parts=1):
-            w = CHUNK // parts
-            cols = slice(n * CHUNK + part * w, n * CHUNK + (part + 1) * w)
-            result = work.tile([P, w], F32, name="result", bufs=8)
+        def pooled_mx(n, jt, role):
+            for g in range(N_GROUPS):
+                pooled_pass(n, jt, g, role, 0, 1)
+
+        def store(n, jt, part, parts):
+            width = CHUNK // parts
+            cols = slice(n * CHUNK + part * width, n * CHUNK + (part + 1) * width)
+            result = work.tile([P, width], F32, name="result", bufs=8)
             nc.vector.tensor_tensor(
                 out=result[:].rearrange("p (c l) -> p c l", l=L),
                 in0=pooled[n, jt, part][:].rearrange("p (l c) -> p c l", l=L),
@@ -364,20 +361,23 @@ def tile_hierarchical_softmax_pooling_f4_kernel(
             )
             nc.sync.dma_start(out=out[jt * P : (jt + 1) * P, cols], in_=result[:])
 
-        warm = keep.tile([P, 1], F32, name="warm")
-        nc.scalar.activation(out=warm[:], in_=ident[:, 0:1], func=ACT.Exp)
-        turn_x(0, 0, ("out", "out"))
-        group_x(0, 0, 0, "scalar")
-        group_x(0, 0, 1, "scalar")
+        def warm_tensor(blocks):
+            idle = bank("mx", [P, blocks, P])
+            nc.tensor.matmul(idle[:], lhsT=ident[:], rhs=ident[:].unsqueeze(1).broadcast_to([P, blocks, P]), start=True, stop=True)
+
+        warm_tensor(4)
+        turn_x(0, 0, "out")
+        group_x(0, 0, ("scalar", "scalar"))
         interleave_w(0, 0, 0, PIECE, "vector")
+        warm_tensor(3)
         turned_bias = bank("sum", [P, P], BF16)
         nc.tensor.transpose(turned_bias[:], bias_rows[:], ident_bf[:])
-        nc.scalar.copy(out=bias[:], in_=turned_bias[:, 0:32])
+        nc.scalar.activation(out=bias[:], in_=turned_bias[:, 0 : CLUSTER_BIAS + 1], func=ACT.Identity)
         quantize_x(0, 0)
         interleave_w(0, 1, 0, PIECE, "vector")
-        turn_x(0, 1, ("z", "z"))
-        group_x(0, 1, 0, "scalar")
-        group_x(0, 1, 1, "vector")
+        turn_x(0, 1, "z")
+        group_x(0, 1, ("scalar", "vector"))
+        warm_tensor(3)
         quantize_w(0)
         quantize_x(0, 1)
         interleave_w(1, 0, 0, PIECE, "scalar")
@@ -388,130 +388,124 @@ def tile_hierarchical_softmax_pooling_f4_kernel(
         word_bias(1)
         quantize_w(1)
         turn_z(0, "z", 0)
-        turn_x(1, 0, ("out", "out"))
+        turn_x(1, 0, "out")
 
         first_pooled = 20
-        late = N_TILES - 4
+        late = N_TILES - TILES
+        first_pool = 12
+        first_gate = 3
         for s in range(N_TILES + 1):
-            u, slot = divmod(s, BLOCKS)
-            gate_g, gate_step = divmod(s - 3, BLOCKS)
-            gate_at = {g: s - 3 - BLOCKS * g for g in range(N_GROUPS)}
+            u, slot = divmod(s, TILES)
+            gate_at = [s - first_gate - TILES * g for g in range(N_GROUPS)]
+            finishing = (slot == 1 and u >= 2) or s == N_TILES
             if s + 2 < N_TILES:
                 word_mx(s + 2)
-            for g in range(N_GROUPS):
-                if gate_at[g] == 0:
-                    logits_mx(("c", g), wc_mx, 0, C, g)
+            if 0 in gate_at:
+                logits_mx(("c", gate_at.index(0)), stage2["wc"], 0, C, gate_at.index(0))
             if first_pooled <= s < late and slot in (0, 1):
                 pooled_mx(0, (s - first_pooled) // 2 + slot, "out")
             if late <= s < N_TILES:
                 pooled_mx(1, s - late, "out")
             if s + 1 < N_TILES:
-                turn_z(s + 1, "z", 1 if s < 20 else 0)
-            if (slot == 1 and u >= 2) or s == N_TILES:
-                turn_inverse(u - 2, False)
+                turn_z(s + 1, "z", 1 if s < first_pooled else 0)
             if slot in (2, 3) and 1 <= u < N_UNITS - 1:
-                sum_words(u - 1, range((slot - 2) * L // 2, (slot - 1) * L // 2), ())
-            if s == N_TILES - 2:
-                sum_words(u - 1, range(L), ())
-            for g in range(N_GROUPS):
-                if gate_at[g] == 1:
-                    turn_z(("c", g), "out")
-            if 12 <= s < 12 + J_TILES:
-                turn_pool(s - 12)
+                sum_words(u - 1, range((slot - 2) * L // 2, (slot - 1) * L // 2))
             if s < N_TILES:
                 word_max(s)
             if s >= 1:
                 word_sub(s - 1)
+            if finishing:
+                turn_inverse(u - 2)
+            if s == N_TILES - 2:
+                sum_words(u - 1, range(L))
+            if 1 in gate_at:
+                turn_z(("c", gate_at.index(1)), "out", 0)
+            if first_pool <= s < first_pool + J_TILES:
+                turn_pool(s - first_pool)
             if 2 <= s <= late:
                 word_exp(s - 2)
             if s >= late:
                 word_exp(s - 1)
             if s + 2 < N_TILES:
                 word_bias(s + 2)
-            piece, part = divmod(s + 11, BLOCKS)
-            if 4 <= piece < 2 * N_CHUNKS:
-                interleave_w(piece, part % 2, (part // 2) * P, P, "scalar")
+            piece, quarter = divmod(s + 11, TILES)
+            if 4 <= piece < N_PIECES:
+                interleave_w(piece, quarter % 2, (quarter // 2) * P, P, "scalar")
             if s == 1:
                 for k in range(N_PASSES):
                     interleave("scalar", wc_grouped[:, k, :, :], wc_raw[:, k, :, :])
-            for g in range(N_GROUPS):
-                if gate_at[g] == 0:
-                    add_bias(("c", g), V // P)
-                if gate_at[g] == 3:
-                    gate_exps(g)
-                if gate_at[g] == 5:
-                    gate_finish(g)
+            if 0 in gate_at:
+                add_bias(("c", gate_at.index(0)), CLUSTER_BIAS)
+            if 3 in gate_at:
+                gate_exps(gate_at.index(3))
+            if 5 in gate_at:
+                gate_finish(gate_at.index(5))
+            if first_pool < s <= first_pool + J_TILES:
+                group_pool(s - 1 - first_pool)
             if s == 0:
-                group_x(1, 0, 0, "vector")
-                group_x(1, 0, 1, "vector")
-                turn_x(1, 1, ("out", "out"))
-                group_x(1, 1, 0, "scalar")
-                group_x(1, 1, 1, "scalar")
+                group_x(1, 0, ("vector", "vector"))
+                turn_x(1, 1, "out")
+                group_x(1, 1, ("scalar", "scalar"))
             if s == 1:
-                quantize_x(1, 0)
-                quantize_x(1, 1)
+                for k in range(N_PASSES):
+                    quantize_x(1, k)
             if s == 2:
-                quantize(wc_mx, wc_grouped[:].rearrange("p k c j -> p (k c j)"))
+                stage2["wc"] = quantize("wc", wc_grouped[:].rearrange("p k c j -> p (k c j)"))
             if 2 <= s < 6:
                 interleave_w(2 + (s - 2) // 2, s % 2, 0, PIECE, "vector")
             if s in (4, 6):
                 quantize_w(s // 2)
-            for g in range(N_GROUPS):
-                if gate_at[g] == 2:
-                    gate_max(g)
-                if gate_at[g] == 4:
-                    gate_invert(g)
-            if 12 < s <= 12 + J_TILES:
-                group_pool(s - 1 - 12, "scalar")
+            if 2 in gate_at:
+                gate_max(gate_at.index(2))
+            if 4 in gate_at:
+                gate_invert(gate_at.index(4))
             if first_pooled <= s < late and slot in (2, 3):
-                store(0, (s - first_pooled - 2) // 2 + slot - 2)
+                store(0, (s - first_pooled - 2) // 2 + slot - 2, 0, 1)
             if late < s < N_TILES:
-                store(1, s - late - 1)
+                store(1, s - late - 1, 0, 1)
             if slot == 0 and 2 <= u < N_UNITS:
                 invert_sums(u - 2)
             if s == N_TILES - 1:
                 invert_sums(u - 1)
-            for g in range(N_GROUPS):
-                if gate_at[g] == 4:
-                    gate_weigh(g)
-            if slot == 1 and 4 <= u + 2 < 2 * N_CHUNKS:
+            if 4 in gate_at:
+                gate_weigh(gate_at.index(4))
+            if slot == 1 and 4 <= u + 2 < N_PIECES:
                 quantize_w(u + 2)
-            if s == 17:
-                quantize(pool_mx, pool_grouped[:].rearrange("p g j u -> p (g j u)").bitcast(BF16))
-            if (slot == 1 and u >= 2) or s == N_TILES:
+            if s == first_pool + J_TILES + 1:
+                stage2["pool"] = quantize("pool", pool_grouped[:].rearrange("p g j u -> p (g j u)").bitcast(BF16))
+            if finishing:
                 if u >= 3:
-                    quantize_h(u - 3)
+                    quantize_h(u - 3, 0)
                 make_factor(u - 2)
                 parts = 2 if s == N_TILES else 1
-                for half in range(parts):
-                    make_h(u - 2, nc.gpsimd, half, parts)
+                for part in range(parts):
+                    make_h(u - 2, nc.gpsimd, part, parts)
 
         last = N_UNITS - 1
         pooled_mx(2, 0, "out")
         pooled_mx(2, 1, "mx")
-        sum_words(last, range(L // 2), ())
         pooled_mx(2, 2, "mx")
-        sum_words(last, range(L // 2, L), ())
+        sum_words(last, range(L))
         pooled_mx(2, 3, "z")
-        store(1, J_TILES - 1)
+        store(1, J_TILES - 1, 0, 1)
         for jt in range(J_TILES - 1):
-            store(2, jt)
+            store(2, jt, 0, 1)
         invert_sums(last)
-        turn_inverse(last, False)
-        store(2, J_TILES - 1)
+        turn_inverse(last)
+        store(2, J_TILES - 1, 0, 1)
         make_factor(last)
-        quantize_h(last - 1, 0, 2)
-        quantize_h(last - 1, 1, 2)
-        tags = (("out", "out", "mx", "mx"), ("z", "z", "z", "sum"))
-        for half in range(2):
+        roles = (("out", "out", "mx", "mx"), ("z", "z", "z", "sum"))
+        for part in range(2):
+            quantize_h(last - 1, part)
+        for part in range(2):
             for jt in range(J_TILES):
-                pooled_pass(3, jt, 0, tags[half][jt], half, 2)
-        make_h(last, nc.vector, 0, 2)
-        make_h(last, nc.vector, 1, 2)
-        for half in range(2):
-            quantize_h(last, half, 2)
+                pooled_pass(3, jt, 0, roles[part][jt], part, 2)
+        for part in range(2):
+            make_h(last, nc.vector, part, 2)
+        for part in range(2):
+            quantize_h(last, part)
             for jt in range(J_TILES):
-                pooled_pass(3, jt, 1, tags[half][jt], half, 2)
-        for half in range(2):
+                pooled_pass(3, jt, 1, roles[part][jt], part, 2)
+        for part in range(2):
             for jt in range(J_TILES):
-                store(3, jt, half, 2)
+                store(3, jt, part, 2)

@@ -72,6 +72,11 @@ def tile_hierarchical_softmax_pooling_f4_kernel(
                 nc.scalar.copy(out=dst, in_=src)
 
         def interleave(engine, dst, src):
+            if engine == "gpsimd":
+                nc.gpsimd.tensor_scalar(
+                    out=dst, in0=src.rearrange("p j c -> p c j"), scalar1=1.0, scalar2=0.0, op0=ALU.mult, op1=ALU.add
+                )
+                return
             copy_on(engine, dst.rearrange("p (c i) j -> p c j i", i=4), src.rearrange("p j (c i) -> p c j i", i=4))
 
         bias_rows = keep.tile([P, P], BF16, name="bias_rows")
@@ -414,6 +419,8 @@ def tile_hierarchical_softmax_pooling_f4_kernel(
                 word_max(s)
             if s >= 1:
                 word_sub(s - 1)
+            if s == N_TILES:
+                warm_tensor(4)
             if finishing:
                 turn_inverse(u - 2)
             if s == N_TILES - 2:
@@ -430,7 +437,7 @@ def tile_hierarchical_softmax_pooling_f4_kernel(
                 word_bias(s + 2)
             piece, quarter = divmod(s + 11, TILES)
             if 4 <= piece < N_PIECES:
-                interleave_w(piece, quarter % 2, (quarter // 2) * P, P, "scalar")
+                interleave_w(piece, quarter % 2, (quarter // 2) * P, P, "gpsimd" if piece == 4 else "scalar")
             if s == 1:
                 for k in range(N_PASSES):
                     interleave("scalar", wc_grouped[:, k, :, :], wc_raw[:, k, :, :])
@@ -451,14 +458,13 @@ def tile_hierarchical_softmax_pooling_f4_kernel(
                     quantize_x(1, k)
             if s == 2:
                 stage2["wc"] = quantize("wc", wc_grouped[:].rearrange("p k c j -> p (k c j)"))
-            if 2 <= s < 6:
-                interleave_w(2 + (s - 2) // 2, s % 2, 0, PIECE, "vector")
+            if 1 <= s < 5:
+                for v0 in range(0, PIECE, P):
+                    interleave_w(2 + (s - 1) // 2, (s - 1) % 2, v0, P, "gpsimd")
             if s in (4, 6):
                 quantize_w(s // 2)
             if 2 in gate_at:
                 gate_max(gate_at.index(2))
-            if 4 in gate_at:
-                gate_invert(gate_at.index(4))
             if first_pooled <= s < late and slot in (2, 3):
                 store(0, (s - first_pooled - 2) // 2 + slot - 2, 0, 1)
             if late < s < N_TILES:
@@ -468,6 +474,7 @@ def tile_hierarchical_softmax_pooling_f4_kernel(
             if s == N_TILES - 1:
                 invert_sums(u - 1)
             if 4 in gate_at:
+                gate_invert(gate_at.index(4))
                 gate_weigh(gate_at.index(4))
             if slot == 1 and 4 <= u + 2 < N_PIECES:
                 quantize_w(u + 2)

from contextlib import ExitStack

import concourse.mybir as mybir
from concourse.masks import make_identity

T, D, C, L, V, J = 1024, 1024, 128, 16, 2048, 512
FLOPS = 2 * T * D * (V + C) + 2 * J * T * V

F32 = mybir.dt.float32
BF16 = mybir.dt.bfloat16
U32 = mybir.dt.uint32
U8 = mybir.dt.uint8
FP8X4 = mybir.dt.float8_e4m3fn_x4
ALU = mybir.AluOpType
ACT = mybir.ActivationFunctionType
AXIS = mybir.AxisListType

P = 128
PACK = 4
PASS = P * PACK
N_PASSES = D // PASS
N_GROUPS = T // PASS
CHUNK = 512
N_CHUNKS = V // CHUNK
TILES = CHUNK // P
N_UNITS = N_CHUNKS * N_GROUPS
N_TILES = N_UNITS * TILES
CHUNK_CLUSTERS = CHUNK // L
TILE_CLUSTERS = P // L
PIECE = CHUNK // 2
N_PIECES = V // PIECE
J_TILES = J // P
CLUSTER_BIAS = V // P
BANKS = {"mx": 2, "z": 3, "sum": 1, "out": 2}


def tile_hierarchical_softmax_pooling_f4_kernel(
    tc, x, w_word, b_word, w_cluster, b_cluster, importance, pool, idf, out
):
    nc = tc.nc
    with ExitStack() as ctx:
        keep = ctx.enter_context(tc.tile_pool(name="keep", bufs=1))
        work = ctx.enter_context(tc.tile_pool(name="work", bufs=2))
        psum = ctx.enter_context(tc.psum_pool(name="psum", bufs=1))
        ctx.enter_context(tc.manual_schedule())

        def bank(role, shape, dtype=F32):
            return psum.tile(shape, dtype, name="bank_" + role, tag=role, bufs=BANKS[role])

        def quantize(name, grouped):
            columns = grouped.shape[1] // PACK
            codes = keep.tile([P, columns], U32, name=name + "_codes", align_bytes=64)
            scales = keep.tile([P, columns], U8, name=name + "_scales", align_bytes=64)
            nc.vector.quantize_mx(out=codes[:].bitcast(FP8X4), scales=scales[:], in_=grouped)
            return codes, scales

        def mx_pass(acc, stationary, m0, moving, first, last):
            nc.tensor.matmul_mx(
                out=acc,
                lhsT=stationary[0][:, m0 : m0 + P].bitcast(FP8X4),
                lhsT_scale=stationary[1][:, m0 : m0 + P],
                rhs=moving[0][:].bitcast(FP8X4),
                rhs_scale=moving[1][:],
                start=first,
                stop=last,
            )

        def copy_on(engine, dst, src):
            if engine == "vector":
                nc.vector.tensor_copy(out=dst, in_=src)
            else:
                nc.scalar.copy(out=dst, in_=src)

        def interleave(engine, dst, src):
            if engine == "gpsimd":
                nc.gpsimd.tensor_scalar(
                    out=dst, in0=src.rearrange("p j c -> p c j"), scalar1=1.0, scalar2=0.0, op0=ALU.mult, op1=ALU.add
                )
                return
            copy_on(engine, dst.rearrange("p (c i) j -> p c j i", i=4), src.rearrange("p j (c i) -> p c j i", i=4))

        bias_rows = keep.tile([P, P], BF16, name="bias_rows")
        nc.gpsimd.memset(bias_rows[:], 0.0)
        ident = keep.tile([P, P], F32, name="ident")
        make_identity(nc, ident[:])
        ident_bf = keep.tile([P, P], BF16, name="ident_bf")
        make_identity(nc, ident_bf[:])

        x_raw = {}
        w_raw = {}

        def load_x(g, k):
            x_raw[g, k] = keep.tile([P, PACK, PASS], BF16, name="x_raw_%d_%d" % (g, k))
            rows = x[g * PASS : (g + 1) * PASS, k * PASS : (k + 1) * PASS]
            nc.sync.dma_start(out=x_raw[g, k][:], in_=rows.rearrange("(p t) d -> p t d", t=PACK))

        def load_w(k, first_piece, pieces):
            raw = keep.tile([P, PACK, pieces * PIECE], BF16, name="w_raw_%d_%d" % (k, first_piece))
            rows = w_word[k * PASS : (k + 1) * PASS, first_piece * PIECE : (first_piece + pieces) * PIECE]
            nc.sync.dma_start(out=raw[:], in_=rows.rearrange("(p j) v -> p j v", j=PACK))
            for r in range(pieces):
                w_raw[k, first_piece + r] = raw[:, :, r * PIECE : (r + 1) * PIECE]

        for k in range(N_PASSES):
            load_x(0, k)
            load_w(k, 0, 1)
        nc.scalar.dma_start(out=bias_rows[0:CLUSTER_BIAS, :], in_=b_word.rearrange("(q p) -> q p", p=P))
        nc.scalar.dma_start(out=bias_rows[CLUSTER_BIAS : CLUSTER_BIAS + 1, :], in_=b_cluster.rearrange("(q p) -> q p", p=P))
        for k in range(N_PASSES):
            load_w(k, 1, 1)
        for k in range(N_PASSES):
            load_x(1, k)
        wc_raw = keep.tile([P, N_PASSES, PACK, C], BF16, name="wc_raw")
        nc.sync.dma_start(
            out=wc_raw[:].rearrange("p k j c -> p k (j c)"),
            in_=w_cluster.rearrange("(k p j) c -> p k (j c)", p=P, j=PACK),
        )
        for k in range(N_PASSES):
            load_w(k, 2, 2)
        imp = keep.tile([P, N_GROUPS, PACK], BF16, name="imp")
        nc.sync.dma_start(out=imp[:], in_=importance.rearrange("(g p t) -> p g t", p=P, t=PACK))
        pool_raw = keep.tile([P, J_TILES, T], BF16, name="pool_raw")
        nc.sync.dma_start(out=pool_raw[:], in_=pool.rearrange("(jt j) t -> j jt t", j=P))
        for k in range(N_PASSES):
            load_w(k, 4, 2)
        idf_rows = keep.tile([P, V], BF16, name="idf_rows")
        nc.sync.dma_start(out=idf_rows[:], in_=idf.partition_broadcast(P))
        for k in range(N_PASSES):
            load_w(k, 6, 2)

        x_turned = {}
        x_grouped = {}
        x_mx = {}

        def turn_x(g, k, role):
            words = x_raw[g, k][:].bitcast(F32)
            for half in range(2):
                x_turned[g, k, half] = bank(role, [P, 2, 2, P])
                for t in range(2):
                    for u in range(2):
                        nc.tensor.transpose(x_turned[g, k, half][:, t, u, :], words[:, 2 * half + t, u::2], ident[:])

        def group_x(g, k, engines):
            x_grouped[g, k] = work.tile([P, PACK, P, 2], F32, name="x_grouped", align_bytes=64)
            for half in range(2):
                copy_on(
                    engines[half],
                    x_grouped[g, k][:, 2 * half : 2 * half + 2, :, :],
                    x_turned[g, k, half][:].rearrange("p t u r -> p t r u"),
                )

        def quantize_x(g, k):
            x_mx[g, k] = quantize("x_%d_%d" % (g, k), x_grouped[g, k][:].rearrange("p t r u -> p (t r u)").bitcast(BF16))

        w_grouped = {}
        w_mx = {}

        def interleave_w(piece, k, v0, width, engine):
            if piece not in w_grouped:
                w_grouped[piece] = work.tile([P, N_PASSES, PIECE, PACK], BF16, name="w_grouped", bufs=3, align_bytes=64)
            interleave(engine, w_grouped[piece][:, k, v0 : v0 + width, :], w_raw[k, piece][:, :, v0 : v0 + width])

        def quantize_w(piece):
            w_mx[piece] = quantize("w_%d" % piece, w_grouped[piece][:].rearrange("p k v j -> p (k v j)"))

        bias = keep.tile([P, CLUSTER_BIAS + 1], F32, name="bias")
        logits = {}
        biased = {}
        turned_z = {}
        top = {}
        shifted = {}
        expd = {}

        def logits_mx(key, stationary, m0, pass_columns, g):
            logits[key] = bank("mx", [P, PASS])
            for k in range(N_PASSES):
                mx_pass(logits[key][:], stationary, m0 + k * pass_columns, x_mx[g, k], k == 0, k == N_PASSES - 1)

        def add_bias(key, column):
            biased[key] = work.tile([P, PASS], F32, name="biased", bufs=3)
            nc.scalar.activation(
                out=biased[key][:], in_=logits[key][:], func=ACT.Identity, bias=bias[:, column : column + 1], scale=1.0
            )

        def turn_z(key, role, products):
            turned_z[key] = bank(role, [P, PACK, P])
            for t in range(PACK):
                nc.tensor.matmul(
                    turned_z[key][:, t, :],
                    lhsT=biased[key][:, t * P : (t + 1) * P],
                    rhs=ident[:],
                    start=True,
                    stop=True,
                    is_transpose=(t < PACK - products),
                )

        def word_mx(i):
            u, q = divmod(i, TILES)
            n, g = divmod(u, N_GROUPS)
            logits_mx(i, w_mx[2 * n + q // 2], (q % 2) * P, PIECE, g)

        def word_bias(i):
            u, q = divmod(i, TILES)
            add_bias(i, (u // N_GROUPS) * TILES + q)

        def word_max(i):
            top[i] = work.tile([P, TILE_CLUSTERS, PACK], F32, name="top", bufs=3)
            nc.vector.tensor_reduce(
                out=top[i][:], in_=turned_z[i][:].rearrange("p t (c l) -> p c t l", l=L), axis=AXIS.X, op=ALU.max
            )

        def word_sub(i):
            shifted[i] = work.tile([P, L, TILE_CLUSTERS, PACK], F32, name="shifted", bufs=3)
            nc.vector.tensor_tensor(
                out=shifted[i][:],
                in0=turned_z[i][:].rearrange("p t (c l) -> p l c t", l=L),
                in1=top[i][:].unsqueeze(1).broadcast_to([P, L, TILE_CLUSTERS, PACK]),
                op=ALU.subtract,
            )

        def word_exp(i):
            u, q = divmod(i, TILES)
            if q == 0:
                expd[u] = work.tile([P, L, P], F32, name="expd", bufs=4)
            width = TILE_CLUSTERS * PACK
            nc.scalar.activation(
                out=expd[u][:, :, q * width : (q + 1) * width],
                in_=shifted[i][:].rearrange("p l c t -> p l (c t)"),
                func=ACT.Exp,
            )

        sums = {}
        upper = {}
        paired = {}
        paired_inv = {}
        inverse = {}
        factor = {}
        gate = {}
        h_grouped = {}
        h_mx = {}
        HALF = P // 2

        def sum_words(u, words):
            if words[0] == 0:
                sums[u] = bank("sum", [P, 2, P])
            for l in words:
                nc.tensor.matmul(
                    sums[u][:, 0, :], lhsT=expd[u][:, l, :], rhs=ident[:], start=(l == 0), stop=(l == L - 1), is_transpose=True
                )

        def invert_sums(u):
            inverse[u] = work.tile([P, P], F32, name="inverse")
            nc.vector.reciprocal(out=inverse[u][:], in_=sums[u][:, 0, :])

        def turn_inverse(u):
            nc.tensor.transpose(sums[u][:, 1, :], inverse[u][:], ident[:])

        def make_factor(u):
            n, g = divmod(u, N_GROUPS)
            factor[u] = work.tile([P, P], F32, name="factor")
            clusters = slice(n * CHUNK_CLUSTERS, (n + 1) * CHUNK_CLUSTERS)
            nc.vector.tensor_tensor(
                out=factor[u][:].rearrange("p (c t) -> p c t", t=PACK),
                in0=sums[u][:, 1, :].rearrange("p (c t) -> p c t", t=PACK),
                in1=gate[g][:, :, clusters].rearrange("p t c -> p c t"),
                op=ALU.mult,
            )

        def make_h(u, engine, part, parts):
            width = P // parts
            h_grouped[u, part] = work.tile([P, L, width], BF16, name="h_grouped", bufs=3, align_bytes=64)
            cols = slice(part * width, (part + 1) * width)
            engine.tensor_tensor(
                out=h_grouped[u, part][:],
                in0=expd[u][:, :, cols],
                in1=factor[u][:, cols].unsqueeze(1).broadcast_to([P, L, width]),
                op=ALU.mult,
            )

        def quantize_h(u, part):
            h_mx[u, part] = quantize("h_%d_%d" % (u, part), h_grouped[u, part][:].rearrange("p l w -> p (l w)"))

        wc_grouped = keep.tile([P, N_PASSES, C, PACK], BF16, name="wc_grouped", align_bytes=64)
        gate_top = {}
        gate_exp = {}
        gate_sum = {}
        gate_inv = {}
        gate_scale = {}

        def gate_max(g):
            gate_top[g] = keep.tile([P, PACK], F32, name="gate_top_%d" % g)
            nc.vector.tensor_reduce(out=gate_top[g][:], in_=turned_z["c", g][:], axis=AXIS.X, op=ALU.max, negate=True)

        def gate_exps(g):
            gate_exp[g] = keep.tile([P, PACK, C], F32, name="gate_exp_%d" % g)
            gate_sum[g] = keep.tile([P, PACK], F32, name="gate_sum_%d" % g)
            for t in range(PACK):
                nc.scalar.activation(
                    out=gate_exp[g][:, t, :],
                    in_=turned_z["c", g][:, t, :],
                    func=ACT.Exp,
                    bias=gate_top[g][:, t : t + 1],
                    scale=1.0,
                    accum_out=gate_sum[g][:, t : t + 1],
                )

        def gate_invert(g):
            gate_inv[g] = keep.tile([P, PACK], F32, name="gate_inv_%d" % g)
            nc.vector.reciprocal(out=gate_inv[g][:], in_=gate_sum[g][:])

        def gate_weigh(g):
            gate_scale[g] = keep.tile([P, PACK], F32, name="gate_scale_%d" % g)
            for t in range(PACK):
                nc.vector.tensor_scalar(
                    out=gate_scale[g][:, t : t + 1],
                    in0=gate_inv[g][:, t : t + 1],
                    scalar1=imp[:, g, t : t + 1],
                    scalar2=float(C * L),
                    op0=ALU.mult,
                    op1=ALU.mult,
                )

        def gate_finish(g):
            gate[g] = keep.tile([P, PACK, C], F32, name="gate_%d" % g)
            for t in range(PACK):
                nc.scalar.activation(
                    out=gate[g][:, t, :], in_=gate_exp[g][:, t, :], func=ACT.Copy, scale=gate_scale[g][:, t : t + 1]
                )

        pool_turned = {}
        pool_grouped = keep.tile([P, N_GROUPS, J, 2], F32, name="pool_grouped", align_bytes=64)

        def turn_pool(jt):
            words = pool_raw[:].bitcast(F32).rearrange("j jt (g w) -> j jt g w", g=N_GROUPS)
            pool_turned[jt] = bank("out", [P, N_GROUPS, 2, P])
            for g in range(N_GROUPS):
                for u in range(2):
                    nc.tensor.transpose(pool_turned[jt][:, g, u, :], words[:, jt, g, u::2], ident[:])

        def group_pool(jt):
            nc.scalar.copy(out=pool_grouped[:, :, jt * P : (jt + 1) * P, :], in_=pool_turned[jt][:].rearrange("p g u r -> p g r u"))

        stage2 = {}
        pooled = {}

        def pooled_pass(n, jt, g, role, part, parts):
            if g == 0:
                pooled[n, jt, part] = bank(role, [P, CHUNK // parts])
            mx_pass(
                pooled[n, jt, part][:], stage2["pool"], g * J + jt * P, h_mx[N_GROUPS * n + g, part], g == 0, g == N_GROUPS - 1
            )

        def pooled_mx(n, jt, role):
            for g in range(N_GROUPS):
                pooled_pass(n, jt, g, role, 0, 1)

        def store(n, jt, part, parts):
            width = CHUNK // parts
            cols = slice(n * CHUNK + part * width, n * CHUNK + (part + 1) * width)
            result = work.tile([P, width], F32, name="result", bufs=8)
            nc.vector.tensor_tensor(
                out=result[:].rearrange("p (c l) -> p c l", l=L),
                in0=pooled[n, jt, part][:].rearrange("p (l c) -> p c l", l=L),
                in1=idf_rows[:, cols].rearrange("p (c l) -> p c l", l=L),
                op=ALU.mult,
            )
            nc.sync.dma_start(out=out[jt * P : (jt + 1) * P, cols], in_=result[:])

        def warm_tensor(blocks):
            idle = bank("mx", [P, blocks, P])
            nc.tensor.matmul(idle[:], lhsT=ident[:], rhs=ident[:].unsqueeze(1).broadcast_to([P, blocks, P]), start=True, stop=True)

        warm_tensor(4)
        turn_x(0, 0, "out")
        group_x(0, 0, ("scalar", "scalar"))
        interleave_w(0, 0, 0, PIECE, "vector")
        warm_tensor(3)
        turned_bias = bank("sum", [P, P], BF16)
        nc.tensor.transpose(turned_bias[:], bias_rows[:], ident_bf[:])
        nc.scalar.activation(out=bias[:], in_=turned_bias[:, 0 : CLUSTER_BIAS + 1], func=ACT.Identity)
        quantize_x(0, 0)
        interleave_w(0, 1, 0, PIECE, "vector")
        turn_x(0, 1, "z")
        group_x(0, 1, ("scalar", "vector"))
        warm_tensor(3)
        quantize_w(0)
        quantize_x(0, 1)
        interleave_w(1, 0, 0, PIECE, "scalar")
        word_mx(0)
        word_mx(1)
        interleave_w(1, 1, 0, PIECE, "vector")
        word_bias(0)
        word_bias(1)
        quantize_w(1)
        turn_z(0, "z", 0)
        turn_x(1, 0, "out")

        first_pooled = 20
        late = N_TILES - TILES
        first_pool = 12
        first_gate = 3
        for s in range(N_TILES + 1):
            u, slot = divmod(s, TILES)
            gate_at = [s - first_gate - TILES * g for g in range(N_GROUPS)]
            finishing = (slot == 1 and u >= 2) or s == N_TILES
            if s + 2 < N_TILES:
                word_mx(s + 2)
            if 0 in gate_at:
                logits_mx(("c", gate_at.index(0)), stage2["wc"], 0, C, gate_at.index(0))
            if first_pooled <= s < late and slot in (0, 1):
                pooled_mx(0, (s - first_pooled) // 2 + slot, "out")
            if late <= s < N_TILES:
                pooled_mx(1, s - late, "out")
            if s + 1 < N_TILES:
                turn_z(s + 1, "z", 1 if s < first_pooled else 0)
            if slot in (2, 3) and 1 <= u < N_UNITS - 1:
                sum_words(u - 1, range((slot - 2) * L // 2, (slot - 1) * L // 2))
            if s < N_TILES:
                word_max(s)
            if s >= 1:
                word_sub(s - 1)
            if s == N_TILES:
                warm_tensor(4)
            if finishing:
                turn_inverse(u - 2)
            if s == N_TILES - 2:
                sum_words(u - 1, range(L))
            if 1 in gate_at:
                turn_z(("c", gate_at.index(1)), "out", 0)
            if first_pool <= s < first_pool + J_TILES:
                turn_pool(s - first_pool)
            if 2 <= s <= late:
                word_exp(s - 2)
            if s >= late:
                word_exp(s - 1)
            if s + 2 < N_TILES:
                word_bias(s + 2)
            piece, quarter = divmod(s + 11, TILES)
            if 4 <= piece < N_PIECES:
                interleave_w(piece, quarter % 2, (quarter // 2) * P, P, "gpsimd" if piece == 4 else "scalar")
            if s == 1:
                for k in range(N_PASSES):
                    interleave("scalar", wc_grouped[:, k, :, :], wc_raw[:, k, :, :])
            if 0 in gate_at:
                add_bias(("c", gate_at.index(0)), CLUSTER_BIAS)
            if 3 in gate_at:
                gate_exps(gate_at.index(3))
            if 5 in gate_at:
                gate_finish(gate_at.index(5))
            if first_pool < s <= first_pool + J_TILES:
                group_pool(s - 1 - first_pool)
            if s == 0:
                group_x(1, 0, ("vector", "vector"))
                turn_x(1, 1, "out")
                group_x(1, 1, ("scalar", "scalar"))
            if s == 1:
                for k in range(N_PASSES):
                    quantize_x(1, k)
            if s == 2:
                stage2["wc"] = quantize("wc", wc_grouped[:].rearrange("p k c j -> p (k c j)"))
            if 1 <= s < 5:
                for v0 in range(0, PIECE, P):
                    interleave_w(2 + (s - 1) // 2, (s - 1) % 2, v0, P, "gpsimd")
            if s in (4, 6):
                quantize_w(s // 2)
            if 2 in gate_at:
                gate_max(gate_at.index(2))
            if first_pooled <= s < late and slot in (2, 3):
                store(0, (s - first_pooled - 2) // 2 + slot - 2, 0, 1)
            if late < s < N_TILES:
                store(1, s - late - 1, 0, 1)
            if slot == 0 and 2 <= u < N_UNITS:
                invert_sums(u - 2)
            if s == N_TILES - 1:
                invert_sums(u - 1)
            if 4 in gate_at:
                gate_invert(gate_at.index(4))
                gate_weigh(gate_at.index(4))
            if slot == 1 and 4 <= u + 2 < N_PIECES:
                quantize_w(u + 2)
            if s == first_pool + J_TILES + 1:
                stage2["pool"] = quantize("pool", pool_grouped[:].rearrange("p g j u -> p (g j u)").bitcast(BF16))
            if finishing:
                if u >= 3:
                    quantize_h(u - 3, 0)
                make_factor(u - 2)
                parts = 2 if s == N_TILES else 1
                for part in range(parts):
                    make_h(u - 2, nc.gpsimd, part, parts)

        last = N_UNITS - 1
        pooled_mx(2, 0, "out")
        pooled_mx(2, 1, "mx")
        pooled_mx(2, 2, "mx")
        sum_words(last, range(L))
        pooled_mx(2, 3, "z")
        store(1, J_TILES - 1, 0, 1)
        for jt in range(J_TILES - 1):
            store(2, jt, 0, 1)
        invert_sums(last)
        turn_inverse(last)
        store(2, J_TILES - 1, 0, 1)
        make_factor(last)
        roles = (("out", "out", "mx", "mx"), ("z", "z", "z", "sum"))
        for part in range(2):
            quantize_h(last - 1, part)
        for part in range(2):
            for jt in range(J_TILES):
                pooled_pass(3, jt, 0, roles[part][jt], part, 2)
        for part in range(2):
            make_h(last, nc.vector, part, 2)
        for part in range(2):
            quantize_h(last, part)
            for jt in range(J_TILES):
                pooled_pass(3, jt, 1, roles[part][jt], part, 2)
        for part in range(2):
            for jt in range(J_TILES):
                store(3, jt, part, 2)
